import numpy as np
import ml_dtypes


def mxq(x, axis, fmt="e4m3"):
    dtype, down = {"e4m3": (ml_dtypes.float8_e4m3fn, 7), "e5m2": (ml_dtypes.float8_e5m2, 14)}[fmt]
    v = np.moveaxis(np.asarray(x, np.float32).astype(ml_dtypes.bfloat16).astype(np.float64), axis, -1)
    blocks = v.reshape(v.shape[:-1] + (-1, 32))
    amax = np.abs(blocks).max(-1, keepdims=True)
    byte = np.maximum(np.where(amax > 0, np.frexp(amax)[1] - 1 + 127, 0) - down, 1)
    scale = np.exp2(byte - 127.0)
    codes = (blocks / scale).astype(np.float32).astype(dtype).astype(np.float64)
    return np.moveaxis((codes * scale).reshape(v.shape), -1, axis)


WIDE = False


def mx_kscale(k):
    if not WIDE:
        return np.ones(k)
    levels = np.array([10, -10, 5, -5, 0])
    if k % 512:
        return np.exp2(np.random.permutation(np.resize(levels, k // 32))).repeat(32)
    a = np.empty((k // 512, 16))
    for p in range(k // 512):
        a[p, :8] = np.random.permutation(np.resize(levels, 8))
        for g in range(8):
            far = levels[np.abs(levels - a[p, g]) >= 10]
            a[p, g + 8] = far[np.random.randint(len(far))]
    return np.exp2(a.ravel()).repeat(32)


def f64(x):
    return np.asarray(x).astype(np.float64)


def striped(idx):
    return np.tile(idx.reshape(-1, 16).T, (8, 1)).astype(np.uint16)


def unstriped(offs):
    return offs[:16].T.reshape(-1).astype(np.int64)


E2M1 = np.array([0.0, 0.5, 1.0, 1.5, 2.0, 3.0, 4.0, 6.0, -0.0, -0.5, -1.0, -1.5, -2.0, -3.0, -4.0, -6.0])


def pack_weight(w, fmt):
    k, n = w.shape
    w = f64(np.asarray(w, np.float32).astype(ml_dtypes.bfloat16)).reshape(k // 32, 32, n)
    amax = np.abs(w).max(1)
    if fmt == "e4m3":
        byte = np.frexp(amax)[1] - 1 + 127 - 7
    else:
        mant, ex = np.frexp(amax / 6.0)
        byte = np.where(mant > 0.5, ex, ex - 1) + 127
    byte = np.clip(np.where(amax > 0, byte, 1), 1, 254)
    scaled = (w * np.exp2(127.0 - byte)[:, None, :]).reshape(k, n).astype(np.float32)
    by_word = np.ascontiguousarray(scaled.reshape(k // 512, 128, 4, n).transpose(0, 1, 3, 2))
    if fmt == "e4m3":
        words = by_word.astype(ml_dtypes.float8_e4m3fn).view(np.uint8)
    else:
        c = by_word.astype(ml_dtypes.float4_e2m1fn).view(np.uint8) & 0xF
        words = (c[..., 0::2] | (c[..., 1::2] << 4)).reshape(k // 512, 128, 2 * n)
    return np.ascontiguousarray(words), np.ascontiguousarray(byte.astype(np.uint8).reshape(k // 512, 16, n))


def unpack_weight(words, scales, fmt):
    g, _, n = scales.shape
    words = np.ascontiguousarray(words).reshape(g, 128, n, -1)
    if fmt == "e4m3":
        vals = words.view(ml_dtypes.float8_e4m3fn).astype(np.float64)
    else:
        nib = np.empty((g, 128, n, 4), np.uint8)
        nib[..., 0::2] = words & 0xF
        nib[..., 1::2] = words >> 4
        vals = E2M1[nib]
    vals = vals * np.repeat(np.exp2(scales.astype(np.float64) - 127.0), 8, axis=1)[..., None]
    return vals.transpose(0, 1, 3, 2).reshape(g * 512, n)


def gelu(v):
    return 0.5 * v * (1.0 + np.tanh(np.sqrt(2.0 / np.pi) * (v + 0.044715 * v**3)))


K, H, T, S, T3, S2 = 1024, 1024, 2048, 512, 2048, 512


def setup_inputs():
    n = np.random.standard_normal
    s = mx_kscale(K)[:, None]
    u = mx_kscale(H)[:, None]
    tab_words, tab_scales = pack_weight(n((K, T)) * s, "e4m3")
    tab2_words, tab2_scales = pack_weight(n((H, T3)) / np.sqrt(H) / u, "e4m3")
    tab3_words, tab3_scales = pack_weight(n((H, T3)) / np.sqrt(H) / u, "e4m3")
    w4_words, w4_scales = pack_weight(1.4 * n((K, H)) / np.sqrt(K) / s, "e2m1")
    return {
        "tab_words": tab_words, "tab_scales": tab_scales,
        "offs": striped(np.random.permutation(T)[:S]),
        "tab2_words": tab2_words, "tab2_scales": tab2_scales,
        "offs2": striped(np.random.permutation(T3)[:S2]),
        "tab3_words": tab3_words, "tab3_scales": tab3_scales,
        "offs3": striped(np.random.permutation(T3)[:S2]),
        "w1": (1.4 * n((K, H)) / np.sqrt(K) / s).astype(np.float32),
        "w4_words": w4_words, "w4_scales": w4_scales,
        "gain1": (1.3 * np.exp(0.3 * n(H)) * u[:, 0]).astype(np.float32),
        "gain2": (np.exp(0.3 * n(H)) * u[:, 0]).astype(np.float32),
        "base": (0.7 * n(S2)).astype(np.float32),
    }


def reference(tab_words, tab_scales, offs, tab2_words, tab2_scales, offs2, tab3_words, tab3_scales, offs3,
              w1, w4_words, w4_scales, gain1, gain2, base):
    v = unpack_weight(tab_words, tab_scales, "e4m3")[:, unstriped(offs)]
    v2 = unpack_weight(tab2_words, tab2_scales, "e4m3")[:, unstriped(offs2)]
    v3 = unpack_weight(tab3_words, tab3_scales, "e4m3")[:, unstriped(offs3)]
    w4 = unpack_weight(w4_words, w4_scales, "e2m1")
    a1 = mxq(f64(w1), 0, "e4m3").T @ v
    h1 = f64(gain1)[:, None] * np.tanh(a1)
    a2 = w4.T @ v
    gelu2 = 0.5 * a2 * (1.0 + np.tanh(0.7978845608028654 * (a2 + 0.044715 * a2 ** 3)))
    h2 = f64(gain2)[:, None] * gelu2
    h1x = mxq(h1, 0, "e4m3")
    h2x = mxq(h2, 0, "e4m3")
    e = v2.T @ h1x + v3.T @ h2x
    f = v2.T @ h2x
    return np.maximum(e, f) + f64(base)[:, None]

@@ -1,0 +1,262 @@
+from contextlib import ExitStack
+
+import concourse.mybir as mybir
+
+K, H, T, S = 1024, 1024, 2048, 512
+FLOPS = 2 * K * H * S * 2 + 2 * H * S * S * 3
+
+F32 = mybir.dt.float32
+BF16 = mybir.dt.bfloat16
+I32 = mybir.dt.int32
+U32 = mybir.dt.uint32
+U16 = mybir.dt.uint16
+U8 = mybir.dt.uint8
+FP8X4 = mybir.dt.float8_e4m3fn_x4
+FP4X4 = mybir.dt.float4_e2m1fn_x4
+ACT = mybir.ActivationFunctionType
+ALU = mybir.AluOpType
+
+P = 128
+PACK = 4
+K_PASS = P * PACK
+PASSES = 2
+HALF = S // 2
+CHUNK = 128
+
+
+def tile_list_theatre_team_scores_kernel(
+    tc, tab_words, tab_scales, offs, tab2_words, tab2_scales, offs2, tab3_words, tab3_scales, offs3,
+    w1, w4_words, w4_scales, gain1, gain2, base, out,
+):
+    nc = tc.nc
+    with ExitStack() as ctx:
+        keep = ctx.enter_context(tc.tile_pool(name="keep", bufs=1))
+        stage = ctx.enter_context(tc.tile_pool(name="stage", bufs=3))
+        ring = ctx.enter_context(tc.psum_pool(name="ring", bufs=4))
+        held = ctx.enter_context(tc.psum_pool(name="held", bufs=1))
+
+        def kept(shape, dtype, name):
+            return keep.tile(shape, dtype, name=name, align_bytes=64)
+
+        lists = [kept([P, S // 16], U16, "list%d" % n) for n in range(3)]
+        words = [[kept([P, T], I32, "words%d_%d" % (n, a)) for a in range(PASSES)] for n in range(3)]
+        v_scales = kept([P, PASSES * T], U8, "v_scales")
+        v2_scales = kept([P, T], U8, "v2_scales")
+        v3_scales = kept([P, T], U8, "v3_scales")
+        w4_raw = kept([P, PASSES, H // 2], I32, "w4_raw")
+        w4_raw_scales = kept([P, PASSES * H], U8, "w4_raw_scales")
+        w1_raw = [[kept([P, PACK, K_PASS], F32, "w1_raw%d_%d" % (a, b)) for b in range(PASSES)] for a in range(PASSES)]
+        gains = [kept([P, PASSES, 8], F32, "gain%d" % n) for n in range(2)]
+        base_col = kept([P, S // P], F32, "base_col")
+
+        nc.vector.memset(v_scales[:].bitcast(I32)[:, 0 : T // 4], 0)
+        nc.gpsimd.memset(v_scales[:].bitcast(I32)[:, T // 4 : T // 2], 0)
+        nc.vector.memset(w4_raw_scales[:].bitcast(I32), 0)
+        nc.gpsimd.memset(v2_scales[:].bitcast(I32), 0)
+        nc.vector.memset(v3_scales[:].bitcast(I32), 0)
+
+        def load_words(n, source, a):
+            nc.sync.dma_start(words[n][a][:], source[a].rearrange("p t i -> p (t i)").bitcast(I32))
+
+        def load_w1(a, b):
+            rows = w1[K_PASS * a : K_PASS * (a + 1), K_PASS * b : K_PASS * (b + 1)]
+            nc.sync.dma_start(w1_raw[a][b][:], rows.rearrange("(p i) c -> p i c", i=PACK))
+
+        def load_gain(n, gain):
+            nc.sync.dma_start(gains[n][:, :, 0:PACK], gain.rearrange("(b p t) -> p b t", b=PASSES, t=PACK))
+
+        def load_planes_side_by_side(queue, tile, source):
+            for r in range(4):
+                queue.dma_start(
+                    tile[:].bitcast(I32)[r:P:32, :].rearrange("q (a t) -> q a t", a=PASSES),
+                    source.bitcast(I32)[:, r:16:4, :].rearrange("a q t -> q a t"),
+                )
+
+        def load_planes_stacked(queue, tile, source, first_row):
+            for q in range(4):
+                queue.dma_start(
+                    tile[:].bitcast(I32)[32 * q + first_row : 32 * q + first_row + 8, :],
+                    source.bitcast(I32)[:, 4 * q : 4 * q + 4, :],
+                )
+
+        V2_ROW, V3_ROW = 4, 8
+        nc.sync.dma_start(lists[0][:], offs)
+        nc.sync.dma_start(w4_raw[:], w4_words.bitcast(I32).rearrange("a p c -> p a c"))
+        nc.sync.dma_start(lists[1][:], offs2)
+        nc.sync.dma_start(lists[2][:], offs3)
+        load_gain(1, gain2)
+        load_planes_side_by_side(nc.sync, v_scales, tab_scales)
+        load_w1(0, 0)
+        load_planes_side_by_side(nc.sync, w4_raw_scales, w4_scales)
+        load_words(0, tab_words, 0)
+        load_planes_stacked(nc.sync, v2_scales, tab2_scales, V2_ROW)
+        load_words(0, tab_words, 1)
+        load_planes_stacked(nc.sync, v3_scales, tab3_scales, V3_ROW)
+        load_w1(1, 0)
+        load_gain(0, gain1)
+        load_w1(0, 1)
+        load_w1(1, 1)
+        with nc.allow_non_contiguous_dma(reason="one offset to a partition"):
+            nc.sync.dma_start(base_col[:], base.rearrange("(c p) -> p c", p=P))
+        load_words(1, tab2_words, 0)
+        load_words(1, tab2_words, 1)
+        load_words(2, tab3_words, 0)
+        load_words(2, tab3_words, 1)
+
+        picked = [[kept([P, S], U32, "picked%d_%d" % (n, a)) for a in range(PASSES)] for n in range(3)]
+        v_planes = [kept([P, S], U8, "v_plane%d" % a) for a in range(PASSES)]
+        v2_planes = kept([P, S], U8, "v2_planes")
+        v3_planes = kept([P, S], U8, "v3_planes")
+
+        def pick_words(n, a):
+            nc.vector.tensor_copy(picked[n][a][:], words[n][a][:].bitcast(U32).indirect(lists[n][:]))
+
+        def pick_plane(dst, window, n):
+            nc.vector.tensor_copy(dst[:], window.indirect(lists[n][:]))
+
+        w4_codes = [kept([P, PASSES, 2 * K_PASS], U8, "w4_codes%d" % b) for b in range(PASSES)]
+        w4_planes = [kept([P, PASSES, K_PASS], U8, "w4_planes%d" % b) for b in range(PASSES)]
+
+        def deal_w4(b):
+            cols = slice(K_PASS * b, K_PASS * (b + 1))
+            nc.vector.tensor_copy(
+                w4_codes[b][:].bitcast(U16).rearrange("p a (t m) -> p a m t", t=PACK),
+                w4_raw[:].bitcast(U16)[:, :, cols].rearrange("p a (m t) -> p a m t", t=PACK),
+            )
+            nc.vector.tensor_copy(
+                w4_planes[b][:].rearrange("p a (t m) -> p a m t", t=PACK),
+                w4_raw_scales[:].rearrange("p (a c) -> p a c", a=PASSES)[:, :, cols].rearrange("p a (m t) -> p a m t", t=PACK),
+            )
+
+        w1_rounded = [[kept([P, PACK * K_PASS], BF16, "w1_rounded%d_%d" % (a, b)) for b in range(PASSES)] for a in range(PASSES)]
+        w1_codes = [[kept([P, K_PASS], U32, "w1_codes%d_%d" % (a, b)) for b in range(PASSES)] for a in range(PASSES)]
+        w1_planes = [[kept([P, K_PASS], U8, "w1_planes%d_%d" % (a, b)) for b in range(PASSES)] for a in range(PASSES)]
+
+        def round_w1(a, b):
+            dst = w1_rounded[a][b][:].rearrange("p (t m i) -> p m i t", t=PACK, i=PACK)
+            src = w1_raw[a][b][:].rearrange("p i (m t) -> p m i t", t=PACK)
+            for m0 in range(0, P, P // 2):
+                nc.scalar.copy(dst[:, m0 : m0 + P // 2], src[:, m0 : m0 + P // 2])
+
+        def quantise_w1(a, b):
+            nc.vector.quantize_mx(w1_codes[a][b][:].bitcast(FP8X4), w1_planes[a][b][:], w1_rounded[a][b][:])
+
+        h_codes = [[kept([P, S], U32, "h_codes%d_%d" % (n, b)) for b in range(PASSES)] for n in range(2)]
+        h_planes = [[kept([P, S], U8, "h_planes%d_%d" % (n, b)) for b in range(PASSES)] for n in range(2)]
+
+        def first_stage(n, b, half):
+            activated = stage.tile([P, HALF, PACK], F32, name="activated", align_bytes=64)
+            for c in range(HALF // CHUNK):
+                cols = slice(HALF * half + CHUNK * c, HALF * half + CHUNK * (c + 1))
+                bank = ring.tile([P, PACK, CHUNK], F32, name="bank")
+                for t in range(PACK):
+                    for a in range(PASSES):
+                        if n == 0:
+                            codes = w1_codes[a][b][:, P * t : P * (t + 1)].bitcast(FP8X4)
+                            plane = w1_planes[a][b][:, P * t : P * (t + 1)]
+                        else:
+                            codes = w4_codes[b][:, a, 2 * P * t : 2 * P * (t + 1)].bitcast(FP4X4)
+                            plane = w4_planes[b][:, a, P * t : P * (t + 1)]
+                        nc.tensor.matmul_mx(
+                            bank[:, t, :], lhsT=codes, lhsT_scale=plane,
+                            rhs=picked[0][a][:, cols].bitcast(FP8X4), rhs_scale=v_planes[a][:, cols],
+                            start=(a == 0), stop=(a == PASSES - 1),
+                        )
+                nc.scalar.activation(
+                    activated[:, CHUNK * c : CHUNK * (c + 1), :], bank[:].rearrange("p t n -> p n t"),
+                    ACT.Tanh if n == 0 else ACT.Gelu_apprx_tanh,
+                )
+            rounded = stage.tile([P, HALF, PACK], BF16, name="rounded", align_bytes=64)
+            nc.vector.tensor_tensor(
+                rounded[:], activated[:],
+                gains[n][:, b, 0:PACK].unsqueeze(1).to_broadcast([P, HALF, PACK]), ALU.mult,
+            )
+            return rounded
+
+        def quantise_h(n, b, half, rounded):
+            cols = slice(HALF * half, HALF * (half + 1))
+            nc.vector.quantize_mx(
+                h_codes[n][b][:, cols].bitcast(FP8X4), h_planes[n][b][:, cols],
+                rounded[:].rearrange("p n t -> p (n t)"),
+            )
+
+        def second_pass(dst, n, b, m, h, cols, start, stop):
+            planes, row = (v2_planes, V2_ROW) if n == 1 else (v3_planes, V3_ROW)
+            teams = slice(P * m, P * (m + 1))
+            nc.tensor.matmul_mx(
+                dst, lhsT=picked[n][b][:, teams].bitcast(FP8X4), lhsT_scale=planes[row + 4 * b : P, teams],
+                rhs=h_codes[h][b][:, cols].bitcast(FP8X4), rhs_scale=h_planes[h][b][:, cols],
+                start=start, stop=stop,
+            )
+
+        for a in range(PASSES):
+            pick_plane(v_planes[a], v_scales[:, T * a : T * (a + 1)], 0)
+        round_w1(0, 0)
+        deal_w4(0)
+        pick_words(0, 0)
+        pick_words(0, 1)
+        deal_w4(1)
+        quantise_w1(0, 0)
+        pick_plane(v2_planes, v2_scales[:], 1)
+        pick_plane(v3_planes, v3_scales[:], 2)
+
+        waiting = []
+
+        def step(n, b, half):
+            rounded = first_stage(n, b, half)
+            if waiting:
+                quantise_h(*waiting.pop())
+            waiting.append((n, b, half, rounded))
+
+        step(1, 0, 0)
+        step(1, 0, 1)
+        round_w1(1, 0)
+        step(1, 1, 0)
+        quantise_w1(1, 0)
+        step(1, 1, 1)
+        step(0, 0, 0)
+        round_w1(0, 1)
+        step(0, 0, 1)
+        round_w1(1, 1)
+        pick_words(1, 0)
+        quantise_h(*waiting.pop())
+        quantise_w1(0, 1)
+        pick_words(1, 1)
+        quantise_w1(1, 1)
+
+        step(0, 1, 0)
+        own = [kept([P, S], F32, "own%d" % m) for m in range(S // P)]
+        for m in range(S // P):
+            bank = ring.tile([P, PACK, CHUNK], F32, name="bank")
+            flat = bank[:].rearrange("p t n -> p (t n)")
+            for b in range(PASSES):
+                second_pass(flat, 1, b, m, 1, slice(0, S), b == 0, b == PASSES - 1)
+            nc.scalar.activation(own[m][:], flat, ACT.Identity, bias=base_col[:, m : m + 1])
+        pick_words(2, 0)
+        step(0, 1, 1)
+        pick_words(2, 1)
+        quantise_h(*waiting.pop())
+
+        joint = [[held.tile([P, 2, HALF], F32, name="joint%d_%d" % (half, g)) for g in range(2)] for half in range(2)]
+        terms = ((1, 0, 0), (2, 0, 1), (2, 1, 1), (1, 1, 0))
+        for k, (n, b, h) in enumerate(terms):
+            for half in range(2):
+                for g in range(2):
+                    for i in range(2):
+                        second_pass(
+                            joint[half][g][:, i, :], n, b, 2 * g + i, h, slice(HALF * half, HALF * (half + 1)),
+                            k == 0 and i == 0, k == len(terms) - 1 and i == 1,
+                        )
+        for half in range(2):
+            cols = slice(HALF * half, HALF * (half + 1))
+            for g in range(2):
+                scores = kept([P, 2, HALF], F32, "scores%d_%d" % (half, g))
+                for i in range(2):
+                    m = 2 * g + i
+                    nc.vector.scalar_tensor_tensor(
+                        scores[:, i, :], joint[half][g][:, i, :], base_col[:, m : m + 1], own[m][:, cols],
+                        ALU.add, ALU.max,
+                    )
+                nc.sync.dma_start(
+                    out[2 * P * g : 2 * P * (g + 1), cols].rearrange("(i p) j -> p i j", p=P), scores[:],
+                )

@@ -31,7 +31,6 @@ def tile_list_theatre_team_scores_kernel(
     nc = tc.nc
     with ExitStack() as ctx:
         keep = ctx.enter_context(tc.tile_pool(name="keep", bufs=1))
-        stage = ctx.enter_context(tc.tile_pool(name="stage", bufs=3))
         ring = ctx.enter_context(tc.psum_pool(name="ring", bufs=4))
         held = ctx.enter_context(tc.psum_pool(name="held", bufs=1))
 
@@ -43,7 +42,7 @@ def tile_list_theatre_team_scores_kernel(
         v_scales = kept([P, PASSES * T], U8, "v_scales")
         v2_scales = kept([P, T], U8, "v2_scales")
         v3_scales = kept([P, T], U8, "v3_scales")
-        w4_raw = kept([P, PASSES, H // 2], I32, "w4_raw")
+        w4_raw = [kept([P, PASSES, K_PASS // 2], I32, "w4_raw%d" % b) for b in range(PASSES)]
         w4_raw_scales = kept([P, PASSES * H], U8, "w4_raw_scales")
         w1_raw = [[kept([P, PACK, K_PASS], F32, "w1_raw%d_%d" % (a, b)) for b in range(PASSES)] for a in range(PASSES)]
         gains = [kept([P, PASSES, 8], F32, "gain%d" % n) for n in range(2)]
@@ -61,6 +60,10 @@ def tile_list_theatre_team_scores_kernel(
         def load_w1(a, b):
             rows = w1[K_PASS * a : K_PASS * (a + 1), K_PASS * b : K_PASS * (b + 1)]
             nc.sync.dma_start(w1_raw[a][b][:], rows.rearrange("(p i) c -> p i c", i=PACK))
+
+        def load_w4(b):
+            cols = slice(K_PASS // 2 * b, K_PASS // 2 * (b + 1))
+            nc.sync.dma_start(w4_raw[b][:], w4_words.bitcast(I32)[:, :, cols].rearrange("a p c -> p a c"))
 
         def load_gain(n, gain):
             nc.sync.dma_start(gains[n][:, :, 0:PACK], gain.rearrange("(b p t) -> p b t", b=PASSES, t=PACK))
@@ -80,48 +83,50 @@ def tile_list_theatre_team_scores_kernel(
                 )
 
         V2_ROW, V3_ROW = 4, 8
+        load_w4(0)
         nc.sync.dma_start(lists[0][:], offs)
-        nc.sync.dma_start(w4_raw[:], w4_words.bitcast(I32).rearrange("a p c -> p a c"))
-        nc.sync.dma_start(lists[1][:], offs2)
-        nc.sync.dma_start(lists[2][:], offs3)
         load_gain(1, gain2)
         load_planes_side_by_side(nc.sync, v_scales, tab_scales)
-        load_w1(0, 0)
-        load_planes_side_by_side(nc.sync, w4_raw_scales, w4_scales)
         load_words(0, tab_words, 0)
-        load_planes_stacked(nc.sync, v2_scales, tab2_scales, V2_ROW)
+        load_planes_side_by_side(nc.sync, w4_raw_scales, w4_scales)
         load_words(0, tab_words, 1)
-        load_planes_stacked(nc.sync, v3_scales, tab3_scales, V3_ROW)
+        nc.sync.dma_start(lists[1][:], offs2)
+        load_w4(1)
+        load_w1(0, 0)
         load_w1(1, 0)
-        load_gain(0, gain1)
+        nc.sync.dma_start(lists[2][:], offs3)
+        load_planes_stacked(nc.sync, v3_scales, tab3_scales, V3_ROW)
         load_w1(0, 1)
-        load_w1(1, 1)
+        load_gain(0, gain1)
+        load_words(1, tab2_words, 0)
         with nc.allow_non_contiguous_dma(reason="one offset to a partition"):
             nc.sync.dma_start(base_col[:], base.rearrange("(c p) -> p c", p=P))
-        load_words(1, tab2_words, 0)
         load_words(1, tab2_words, 1)
+        load_w1(1, 1)
         load_words(2, tab3_words, 0)
         load_words(2, tab3_words, 1)
+        load_planes_stacked(nc.gpsimd, v2_scales, tab2_scales, V2_ROW)
 
-        picked = [[kept([P, S], U32, "picked%d_%d" % (n, a)) for a in range(PASSES)] for n in range(3)]
+        picked = {}
         v_planes = [kept([P, S], U8, "v_plane%d" % a) for a in range(PASSES)]
-        v2_planes = kept([P, S], U8, "v2_planes")
-        v3_planes = kept([P, S], U8, "v3_planes")
+        v2_planes = kept([P, S], U8, "w4_raw_scales")
+        v3_planes = kept([P, S], U8, "v2_scales")
 
-        def pick_words(n, a):
-            nc.vector.tensor_copy(picked[n][a][:], words[n][a][:].bitcast(U32).indirect(lists[n][:]))
+        def pick_words(n, a, slot):
+            picked[n, a] = kept([P, S], U32, slot)
+            nc.vector.tensor_copy(picked[n, a][:], words[n][a][:].bitcast(U32).indirect(lists[n][:]))
 
         def pick_plane(dst, window, n):
             nc.vector.tensor_copy(dst[:], window.indirect(lists[n][:]))
 
         w4_codes = [kept([P, PASSES, 2 * K_PASS], U8, "w4_codes%d" % b) for b in range(PASSES)]
-        w4_planes = [kept([P, PASSES, K_PASS], U8, "w4_planes%d" % b) for b in range(PASSES)]
+        w4_planes = [kept([P, PASSES, K_PASS], U8, "w4_planes0"), kept([P, PASSES, K_PASS], U8, "words0_1")]
 
         def deal_w4(b):
             cols = slice(K_PASS * b, K_PASS * (b + 1))
             nc.vector.tensor_copy(
                 w4_codes[b][:].bitcast(U16).rearrange("p a (t m) -> p a m t", t=PACK),
-                w4_raw[:].bitcast(U16)[:, :, cols].rearrange("p a (m t) -> p a m t", t=PACK),
+                w4_raw[b][:].bitcast(U16).rearrange("p a (m t) -> p a m t", t=PACK),
             )
             nc.vector.tensor_copy(
                 w4_planes[b][:].rearrange("p a (t m) -> p a m t", t=PACK),
@@ -129,44 +134,46 @@ def tile_list_theatre_team_scores_kernel(
             )
 
         w1_rounded = [[kept([P, PACK * K_PASS], BF16, "w1_rounded%d_%d" % (a, b)) for b in range(PASSES)] for a in range(PASSES)]
-        w1_codes = [[kept([P, K_PASS], U32, "w1_codes%d_%d" % (a, b)) for b in range(PASSES)] for a in range(PASSES)]
+        w1_codes = {}
         w1_planes = [[kept([P, K_PASS], U8, "w1_planes%d_%d" % (a, b)) for b in range(PASSES)] for a in range(PASSES)]
 
-        def round_w1(a, b):
+        def round_w1(a, b, part):
             dst = w1_rounded[a][b][:].rearrange("p (t m i) -> p m i t", t=PACK, i=PACK)
             src = w1_raw[a][b][:].rearrange("p i (m t) -> p m i t", t=PACK)
-            for m0 in range(0, P, P // 2):
-                nc.scalar.copy(dst[:, m0 : m0 + P // 2], src[:, m0 : m0 + P // 2])
+            m0 = part * P // 2
+            nc.scalar.copy(dst[:, m0 : m0 + P // 2], src[:, m0 : m0 + P // 2])
 
-        def quantise_w1(a, b):
-            nc.vector.quantize_mx(w1_codes[a][b][:].bitcast(FP8X4), w1_planes[a][b][:], w1_rounded[a][b][:])
+        def quantise_w1(a, b, slot):
+            w1_codes[a, b] = kept([P, K_PASS], U32, slot)
+            nc.vector.quantize_mx(w1_codes[a, b][:].bitcast(FP8X4), w1_planes[a][b][:], w1_rounded[a][b][:])
 
         h_codes = [[kept([P, S], U32, "h_codes%d_%d" % (n, b)) for b in range(PASSES)] for n in range(2)]
         h_planes = [[kept([P, S], U8, "h_planes%d_%d" % (n, b)) for b in range(PASSES)] for n in range(2)]
 
-        def first_stage(n, b, half):
-            activated = stage.tile([P, HALF, PACK], F32, name="activated", align_bytes=64)
+        def first_stage(n, b, half, slot):
+            activated = kept([P, HALF, PACK], F32, "activated%d_%d_%d" % (n, b, half))
+            passes = (1, 0) if (n, b) == (0, 1) else (0, 1)
             for c in range(HALF // CHUNK):
                 cols = slice(HALF * half + CHUNK * c, HALF * half + CHUNK * (c + 1))
                 bank = ring.tile([P, PACK, CHUNK], F32, name="bank")
-                for t in range(PACK):
-                    for a in range(PASSES):
+                for a in passes:
+                    for t in range(PACK):
                         if n == 0:
-                            codes = w1_codes[a][b][:, P * t : P * (t + 1)].bitcast(FP8X4)
+                            codes = w1_codes[a, b][:, P * t : P * (t + 1)].bitcast(FP8X4)
                             plane = w1_planes[a][b][:, P * t : P * (t + 1)]
                         else:
                             codes = w4_codes[b][:, a, 2 * P * t : 2 * P * (t + 1)].bitcast(FP4X4)
                             plane = w4_planes[b][:, a, P * t : P * (t + 1)]
                         nc.tensor.matmul_mx(
                             bank[:, t, :], lhsT=codes, lhsT_scale=plane,
-                            rhs=picked[0][a][:, cols].bitcast(FP8X4), rhs_scale=v_planes[a][:, cols],
-                            start=(a == 0), stop=(a == PASSES - 1),
+                            rhs=picked[0, a][:, cols].bitcast(FP8X4), rhs_scale=v_planes[a][:, cols],
+                            start=(a == passes[0] and t == 0), stop=(a == passes[-1] and t == PACK - 1),
                         )
                 nc.scalar.activation(
                     activated[:, CHUNK * c : CHUNK * (c + 1), :], bank[:].rearrange("p t n -> p n t"),
                     ACT.Tanh if n == 0 else ACT.Gelu_apprx_tanh,
                 )
-            rounded = stage.tile([P, HALF, PACK], BF16, name="rounded", align_bytes=64)
+            rounded = kept([P, HALF, PACK], BF16, slot)
             nc.vector.tensor_tensor(
                 rounded[:], activated[:],
                 gains[n][:, b, 0:PACK].unsqueeze(1).to_broadcast([P, HALF, PACK]), ALU.mult,
@@ -184,69 +191,82 @@ def tile_list_theatre_team_scores_kernel(
             planes, row = (v2_planes, V2_ROW) if n == 1 else (v3_planes, V3_ROW)
             teams = slice(P * m, P * (m + 1))
             nc.tensor.matmul_mx(
-                dst, lhsT=picked[n][b][:, teams].bitcast(FP8X4), lhsT_scale=planes[row + 4 * b : P, teams],
+                dst, lhsT=picked[n, b][:, teams].bitcast(FP8X4), lhsT_scale=planes[row + 4 * b : P, teams],
                 rhs=h_codes[h][b][:, cols].bitcast(FP8X4), rhs_scale=h_planes[h][b][:, cols],
                 start=start, stop=stop,
             )
 
-        for a in range(PASSES):
-            pick_plane(v_planes[a], v_scales[:, T * a : T * (a + 1)], 0)
-        round_w1(0, 0)
-        deal_w4(0)
-        pick_words(0, 0)
-        pick_words(0, 1)
-        deal_w4(1)
-        quantise_w1(0, 0)
-        pick_plane(v2_planes, v2_scales[:], 1)
-        pick_plane(v3_planes, v3_scales[:], 2)
-
         waiting = []
 
-        def step(n, b, half):
-            rounded = first_stage(n, b, half)
+        def step(n, b, half, slot):
+            rounded = first_stage(n, b, half, slot)
             if waiting:
                 quantise_h(*waiting.pop())
             waiting.append((n, b, half, rounded))
 
-        step(1, 0, 0)
-        step(1, 0, 1)
-        round_w1(1, 0)
-        step(1, 1, 0)
-        quantise_w1(1, 0)
-        step(1, 1, 1)
-        step(0, 0, 0)
-        round_w1(0, 1)
-        step(0, 0, 1)
-        round_w1(1, 1)
-        pick_words(1, 0)
-        quantise_h(*waiting.pop())
-        quantise_w1(0, 1)
-        pick_words(1, 1)
-        quantise_w1(1, 1)
 
-        step(0, 1, 0)
-        own = [kept([P, S], F32, "own%d" % m) for m in range(S // P)]
-        for m in range(S // P):
+        def own_score(m):
             bank = ring.tile([P, PACK, CHUNK], F32, name="bank")
             flat = bank[:].rearrange("p t n -> p (t n)")
             for b in range(PASSES):
                 second_pass(flat, 1, b, m, 1, slice(0, S), b == 0, b == PASSES - 1)
-            nc.scalar.activation(own[m][:], flat, ACT.Identity, bias=base_col[:, m : m + 1])
-        pick_words(2, 0)
-        step(0, 1, 1)
-        pick_words(2, 1)
-        quantise_h(*waiting.pop())
+            nc.scalar.activation(own[:, m, :], flat, ACT.Identity, bias=base_col[:, m : m + 1])
 
         joint = [[held.tile([P, 2, HALF], F32, name="joint%d_%d" % (half, g)) for g in range(2)] for half in range(2)]
-        terms = ((1, 0, 0), (2, 0, 1), (2, 1, 1), (1, 1, 0))
-        for k, (n, b, h) in enumerate(terms):
+
+        def joint_term(n, b, h, half, first, last):
+            for g in range(2):
+                for i in range(2):
+                    second_pass(
+                        joint[half][g][:, i, :], n, b, 2 * g + i, h, slice(HALF * half, HALF * (half + 1)),
+                        first and i == 0, last and i == 1,
+                    )
+
+        pick_words(0, 0, "picked0_0")
+        pick_plane(v_planes[0], v_scales[:, 0:T], 0)
+        deal_w4(0)
+        pick_plane(v_planes[1], v_scales[:, T : 2 * T], 0)
+        pick_words(0, 1, "picked0_1")
+        deal_w4(1)
+        pick_plane(v2_planes, v2_scales[:], 1)
+        step(1, 0, 0, "rounded0")
+        round_w1(0, 0, 0)
+        step(1, 0, 1, "rounded1")
+        round_w1(0, 0, 1)
+        quantise_w1(0, 0, "w1_codes0_0")
+        pick_plane(v3_planes, v3_scales[:], 2)
+        step(1, 1, 0, "rounded2")
+        round_w1(1, 0, 0)
+        step(1, 1, 1, "rounded3")
+        round_w1(1, 0, 1)
+        quantise_w1(1, 0, "w1_codes1_0")
+        round_w1(0, 1, 0)
+        round_w1(0, 1, 1)
+        pick_words(1, 0, "picked1_0")
+        quantise_w1(0, 1, "words1_0")
+        pick_words(1, 1, "picked1_1")
+        step(0, 0, 0, "words1_1")
+        step(0, 0, 1, "activated0_0_0")
+        round_w1(1, 1, 0)
+        round_w1(1, 1, 1)
+        own = kept([P, S // P, S], F32, "w1_raw1_1")
+        for m in range(S // P):
+            own_score(m)
+        quantise_h(*waiting.pop())
+        for half in range(2):
+            joint_term(1, 0, 0, half, True, False)
+        quantise_w1(1, 1, "w1_codes1_1")
+        pick_words(2, 0, "picked2_0")
+        pick_words(2, 1, "picked2_1")
+        step(0, 1, 0, "words2_1")
+        step(0, 1, 1, "activated0_1_0")
+        quantise_h(*waiting.pop())
+        for b in range(PASSES):
             for half in range(2):
-                for g in range(2):
-                    for i in range(2):
-                        second_pass(
-                            joint[half][g][:, i, :], n, b, 2 * g + i, h, slice(HALF * half, HALF * (half + 1)),
-                            k == 0 and i == 0, k == len(terms) - 1 and i == 1,
-                        )
+                joint_term(2, b, 1, half, False, False)
+        for half in range(2):
+            joint_term(1, 1, 0, half, False, True)
+
         for half in range(2):
             cols = slice(HALF * half, HALF * (half + 1))
             for g in range(2):
@@ -254,7 +274,7 @@ def tile_list_theatre_team_scores_kernel(
                 for i in range(2):
                     m = 2 * g + i
                     nc.vector.scalar_tensor_tensor(
-                        scores[:, i, :], joint[half][g][:, i, :], base_col[:, m : m + 1], own[m][:, cols],
+                        scores[:, i, :], joint[half][g][:, i, :], base_col[:, m : m + 1], own[:, m, cols],
                         ALU.add, ALU.max,
                     )
                 nc.sync.dma_start(

@@ -1,6 +1,7 @@
 from contextlib import ExitStack
 
 import concourse.mybir as mybir
+from concourse.masks import make_identity
 
 K, H, T, S = 1024, 1024, 2048, 512
 FLOPS = 2 * K * H * S * 2 + 2 * H * S * S * 3
@@ -22,6 +23,7 @@ K_PASS = P * PACK
 PASSES = 2
 HALF = S // 2
 CHUNK = 128
+SPLIT = 64
 
 
 def tile_list_theatre_team_scores_kernel(
@@ -31,7 +33,7 @@ def tile_list_theatre_team_scores_kernel(
     nc = tc.nc
     with ExitStack() as ctx:
         keep = ctx.enter_context(tc.tile_pool(name="keep", bufs=1))
-        ring = ctx.enter_context(tc.psum_pool(name="ring", bufs=4))
+        ring = ctx.enter_context(tc.psum_pool(name="ring", bufs=1))
         held = ctx.enter_context(tc.psum_pool(name="held", bufs=1))
 
         def kept(shape, dtype, name):
@@ -44,29 +46,32 @@ def tile_list_theatre_team_scores_kernel(
         v3_scales = kept([P, T], U8, "v3_scales")
         w4_raw = [kept([P, PASSES, K_PASS // 2], I32, "w4_raw%d" % b) for b in range(PASSES)]
         w4_raw_scales = kept([P, PASSES * H], U8, "w4_raw_scales")
-        w1_raw = [[kept([P, PACK, K_PASS], F32, "w1_raw%d_%d" % (a, b)) for b in range(PASSES)] for a in range(PASSES)]
-        gains = [kept([P, PASSES, 8], F32, "gain%d" % n) for n in range(2)]
+        w1_raw = [kept([P, PACK, H], F32, "w1_raw%d" % a) for a in range(PASSES)]
+        vectors = kept([P, K_PASS], F32, "vectors")
+        identity = kept([P, P], F32, "identity")
+        gains = kept([P, 2 * PASSES, PACK], F32, "gains")
         base_col = kept([P, S // P], F32, "base_col")
 
         nc.vector.memset(v_scales[:].bitcast(I32)[:, 0 : T // 4], 0)
         nc.gpsimd.memset(v_scales[:].bitcast(I32)[:, T // 4 : T // 2], 0)
+        nc.vector.memset(vectors[:], 0.0)
         nc.vector.memset(w4_raw_scales[:].bitcast(I32), 0)
+        make_identity(nc, identity[:])
         nc.gpsimd.memset(v2_scales[:].bitcast(I32), 0)
         nc.vector.memset(v3_scales[:].bitcast(I32), 0)
 
         def load_words(n, source, a):
             nc.sync.dma_start(words[n][a][:], source[a].rearrange("p t i -> p (t i)").bitcast(I32))
 
-        def load_w1(a, b):
-            rows = w1[K_PASS * a : K_PASS * (a + 1), K_PASS * b : K_PASS * (b + 1)]
-            nc.sync.dma_start(w1_raw[a][b][:], rows.rearrange("(p i) c -> p i c", i=PACK))
+        def load_w1(a):
+            nc.sync.dma_start(w1_raw[a][:], w1[K_PASS * a : K_PASS * (a + 1), :].rearrange("(p i) c -> p i c", i=PACK))
 
         def load_w4(b):
             cols = slice(K_PASS // 2 * b, K_PASS // 2 * (b + 1))
             nc.sync.dma_start(w4_raw[b][:], w4_words.bitcast(I32)[:, :, cols].rearrange("a p c -> p a c"))
 
         def load_gain(n, gain):
-            nc.sync.dma_start(gains[n][:, :, 0:PACK], gain.rearrange("(b p t) -> p b t", b=PASSES, t=PACK))
+            nc.sync.dma_start(vectors[PASSES * n : PASSES * (n + 1), :], gain.rearrange("(b c) -> b c", b=PASSES))
 
         def load_planes_side_by_side(queue, tile, source):
             for r in range(4):
@@ -83,34 +88,37 @@ def tile_list_theatre_team_scores_kernel(
                 )
 
         V2_ROW, V3_ROW = 4, 8
+        BASE_ROW = 2 * PASSES
         load_w4(0)
         nc.sync.dma_start(lists[0][:], offs)
-        load_gain(1, gain2)
+        load_w4(1)
         load_planes_side_by_side(nc.sync, v_scales, tab_scales)
         load_words(0, tab_words, 0)
+        load_gain(1, gain2)
+        load_gain(0, gain1)
         load_planes_side_by_side(nc.sync, w4_raw_scales, w4_scales)
         load_words(0, tab_words, 1)
+
+        turned = held.tile([P, PACK, P], F32, name="held0")
+        for t in range(PACK):
+            nc.tensor.transpose(turned[:, t, :], vectors[:, t:K_PASS:PACK], identity[:])
+        nc.vector.tensor_copy(gains[:], turned[:, :, 0:BASE_ROW].rearrange("p t r -> p r t"))
+
         nc.sync.dma_start(lists[1][:], offs2)
-        load_w4(1)
-        load_w1(0, 0)
-        load_w1(1, 0)
+        load_w1(0)
         nc.sync.dma_start(lists[2][:], offs3)
-        load_planes_stacked(nc.sync, v3_scales, tab3_scales, V3_ROW)
-        load_w1(0, 1)
-        load_gain(0, gain1)
+        nc.sync.dma_start(vectors[BASE_ROW : BASE_ROW + 1, :], base.rearrange("(o c) -> o c", o=1))
+        load_w1(1)
         load_words(1, tab2_words, 0)
-        with nc.allow_non_contiguous_dma(reason="one offset to a partition"):
-            nc.sync.dma_start(base_col[:], base.rearrange("(c p) -> p c", p=P))
         load_words(1, tab2_words, 1)
-        load_w1(1, 1)
         load_words(2, tab3_words, 0)
         load_words(2, tab3_words, 1)
         load_planes_stacked(nc.gpsimd, v2_scales, tab2_scales, V2_ROW)
+        load_planes_stacked(nc.gpsimd, v3_scales, tab3_scales, V3_ROW)
 
         picked = {}
         v_planes = [kept([P, S], U8, "v_plane%d" % a) for a in range(PASSES)]
         v2_planes = kept([P, S], U8, "w4_raw_scales")
-        v3_planes = kept([P, S], U8, "v2_scales")
 
         def pick_words(n, a, slot):
             picked[n, a] = kept([P, S], U32, slot)
@@ -134,14 +142,15 @@ def tile_list_theatre_team_scores_kernel(
             )
 
         w1_rounded = [[kept([P, PACK * K_PASS], BF16, "w1_rounded%d_%d" % (a, b)) for b in range(PASSES)] for a in range(PASSES)]
+        v3_planes = kept([P, S], U8, "w1_rounded0_0")
         w1_codes = {}
         w1_planes = [[kept([P, K_PASS], U8, "w1_planes%d_%d" % (a, b)) for b in range(PASSES)] for a in range(PASSES)]
 
-        def round_w1(a, b, part):
-            dst = w1_rounded[a][b][:].rearrange("p (t m i) -> p m i t", t=PACK, i=PACK)
-            src = w1_raw[a][b][:].rearrange("p i (m t) -> p m i t", t=PACK)
-            m0 = part * P // 2
-            nc.scalar.copy(dst[:, m0 : m0 + P // 2], src[:, m0 : m0 + P // 2])
+        def round_w1(a, b, part, copy):
+            copy(
+                w1_rounded[a][b][:].rearrange("p (t m i) -> p m i t", t=PACK, i=PACK)[:, part],
+                w1_raw[a][:, :, K_PASS * b : K_PASS * (b + 1)].rearrange("p i (m t) -> p m i t", t=PACK)[:, part],
+            )
 
         def quantise_w1(a, b, slot):
             w1_codes[a, b] = kept([P, K_PASS], U32, slot)
@@ -152,10 +161,10 @@ def tile_list_theatre_team_scores_kernel(
 
         def first_stage(n, b, half, slot):
             activated = kept([P, HALF, PACK], F32, "activated%d_%d_%d" % (n, b, half))
-            passes = (1, 0) if (n, b) == (0, 1) else (0, 1)
+            passes = (1, 0) if (n, b, half) == (1, 0, 1) else (0, 1)
             for c in range(HALF // CHUNK):
                 cols = slice(HALF * half + CHUNK * c, HALF * half + CHUNK * (c + 1))
-                bank = ring.tile([P, PACK, CHUNK], F32, name="bank")
+                bank = ring.tile([P, PACK, CHUNK], F32, name="bank%d" % (2 * half + c))
                 for a in passes:
                     for t in range(PACK):
                         if n == 0:
@@ -176,7 +185,7 @@ def tile_list_theatre_team_scores_kernel(
             rounded = kept([P, HALF, PACK], BF16, slot)
             nc.vector.tensor_tensor(
                 rounded[:], activated[:],
-                gains[n][:, b, 0:PACK].unsqueeze(1).to_broadcast([P, HALF, PACK]), ALU.mult,
+                gains[:, PASSES * n + b, :].unsqueeze(1).to_broadcast([P, HALF, PACK]), ALU.mult,
             )
             return rounded
 
@@ -206,13 +215,12 @@ def tile_list_theatre_team_scores_kernel(
 
 
         def own_score(m):
-            bank = ring.tile([P, PACK, CHUNK], F32, name="bank")
-            flat = bank[:].rearrange("p t n -> p (t n)")
+            bank = held.tile([P, S], F32, name="held%d" % m)
+            flat = bank[:]
             for b in range(PASSES):
                 second_pass(flat, 1, b, m, 1, slice(0, S), b == 0, b == PASSES - 1)
             nc.scalar.activation(own[:, m, :], flat, ACT.Identity, bias=base_col[:, m : m + 1])
 
-        joint = [[held.tile([P, 2, HALF], F32, name="joint%d_%d" % (half, g)) for g in range(2)] for half in range(2)]
 
         def joint_term(n, b, h, half, first, last):
             for g in range(2):
@@ -229,43 +237,43 @@ def tile_list_theatre_team_scores_kernel(
         pick_words(0, 1, "picked0_1")
         deal_w4(1)
         pick_plane(v2_planes, v2_scales[:], 1)
-        step(1, 0, 0, "rounded0")
-        round_w1(0, 0, 0)
-        step(1, 0, 1, "rounded1")
-        round_w1(0, 0, 1)
-        quantise_w1(0, 0, "w1_codes0_0")
-        pick_plane(v3_planes, v3_scales[:], 2)
-        step(1, 1, 0, "rounded2")
-        round_w1(1, 0, 0)
-        step(1, 1, 1, "rounded3")
-        round_w1(1, 0, 1)
-        quantise_w1(1, 0, "w1_codes1_0")
-        round_w1(0, 1, 0)
-        round_w1(0, 1, 1)
-        pick_words(1, 0, "picked1_0")
-        quantise_w1(0, 1, "words1_0")
-        pick_words(1, 1, "picked1_1")
-        step(0, 0, 0, "words1_1")
-        step(0, 0, 1, "activated0_0_0")
-        round_w1(1, 1, 0)
-        round_w1(1, 1, 1)
-        own = kept([P, S // P, S], F32, "w1_raw1_1")
-        for m in range(S // P):
-            own_score(m)
-        quantise_h(*waiting.pop())
-        for half in range(2):
-            joint_term(1, 0, 0, half, True, False)
-        quantise_w1(1, 1, "w1_codes1_1")
-        pick_words(2, 0, "picked2_0")
-        pick_words(2, 1, "picked2_1")
-        step(0, 1, 0, "words2_1")
-        step(0, 1, 1, "activated0_1_0")
-        quantise_h(*waiting.pop())
         for b in range(PASSES):
             for half in range(2):
-                joint_term(2, b, 1, half, False, False)
-        for half in range(2):
-            joint_term(1, 1, 0, half, False, True)
+                step(1, b, half, "rounded%d_%d" % (b, half))
+        quantise_h(*waiting.pop())
+
+        turned = held.tile([P, S // P, P], F32, name="held1")
+        for m in range(S // P):
+            nc.tensor.transpose(turned[:, m, :], vectors[:, P * m : P * (m + 1)], identity[:])
+        nc.vector.tensor_copy(base_col[:], turned[:, :, BASE_ROW])
+
+        round_w1(0, 0, slice(0, P), nc.scalar.copy)
+        quantise_w1(0, 0, "w1_codes0_0")
+        pick_plane(v3_planes, v3_scales[:], 2)
+        round_w1(0, 1, slice(0, P), nc.scalar.copy)
+        pick_words(1, 0, "picked1_0")
+        quantise_w1(0, 1, "words1_0")
+        round_w1(1, 0, slice(0, SPLIT), nc.scalar.copy)
+        round_w1(1, 0, slice(SPLIT, P), nc.vector.tensor_copy)
+        pick_words(1, 1, "picked1_1")
+        quantise_w1(1, 0, "words1_1")
+        round_w1(1, 1, slice(0, P), nc.scalar.copy)
+        own = kept([P, S // P, S], F32, "own")
+        for m in range(S // P):
+            own_score(m)
+        joint = [[held.tile([P, 2, HALF], F32, name="held%d" % (2 * half + g)) for g in range(2)] for half in range(2)]
+        pick_words(2, 0, "picked2_0")
+        quantise_w1(1, 1, "words2_0")
+        pick_words(2, 1, "picked2_1")
+        step(0, 0, 0, "words2_1")
+        step(0, 0, 1, "activated0_0_0")
+        step(0, 1, 0, "activated0_0_1")
+        step(0, 1, 1, "activated0_1_0")
+        quantise_h(*waiting.pop())
+        terms = ((2, 0, 1), (2, 1, 1), (1, 0, 0), (1, 1, 0))
+        for k, (n, b, h) in enumerate(terms):
+            for half in range(2):
+                joint_term(n, b, h, half, k == 0, k == len(terms) - 1)
 
         for half in range(2):
             cols = slice(HALF * half, HALF * (half + 1))

from contextlib import ExitStack

import concourse.mybir as mybir
from concourse.masks import make_identity

K, H, T, S = 1024, 1024, 2048, 512
FLOPS = 2 * K * H * S * 2 + 2 * H * S * S * 3

F32 = mybir.dt.float32
BF16 = mybir.dt.bfloat16
I32 = mybir.dt.int32
U32 = mybir.dt.uint32
U16 = mybir.dt.uint16
U8 = mybir.dt.uint8
FP8X4 = mybir.dt.float8_e4m3fn_x4
FP4X4 = mybir.dt.float4_e2m1fn_x4
ACT = mybir.ActivationFunctionType
ALU = mybir.AluOpType

P = 128
PACK = 4
K_PASS = P * PACK
PASSES = 2
HALF = S // 2
CHUNK = 128
SPLIT = 64


def tile_list_theatre_team_scores_kernel(
    tc, tab_words, tab_scales, offs, tab2_words, tab2_scales, offs2, tab3_words, tab3_scales, offs3,
    w1, w4_words, w4_scales, gain1, gain2, base, out,
):
    nc = tc.nc
    with ExitStack() as ctx:
        keep = ctx.enter_context(tc.tile_pool(name="keep", bufs=1))
        ring = ctx.enter_context(tc.psum_pool(name="ring", bufs=1))
        held = ctx.enter_context(tc.psum_pool(name="held", bufs=1))

        def kept(shape, dtype, name):
            return keep.tile(shape, dtype, name=name, align_bytes=64)

        lists = [kept([P, S // 16], U16, "list%d" % n) for n in range(3)]
        words = [[kept([P, T], I32, "words%d_%d" % (n, a)) for a in range(PASSES)] for n in range(3)]
        v_scales = kept([P, PASSES * T], U8, "v_scales")
        v2_scales = kept([P, T], U8, "v2_scales")
        v3_scales = kept([P, T], U8, "v3_scales")
        w4_raw = [kept([P, PASSES, K_PASS // 2], I32, "w4_raw%d" % b) for b in range(PASSES)]
        w4_raw_scales = kept([P, PASSES * H], U8, "w4_raw_scales")
        w1_raw = [kept([P, PACK, H], F32, "w1_raw%d" % a) for a in range(PASSES)]
        vectors = kept([P, K_PASS], F32, "vectors")
        identity = kept([P, P], F32, "identity")
        gains = kept([P, 2 * PASSES, PACK], F32, "gains")
        base_col = kept([P, S // P], F32, "base_col")

        nc.vector.memset(v_scales[:].bitcast(I32)[:, 0 : T // 4], 0)
        nc.gpsimd.memset(v_scales[:].bitcast(I32)[:, T // 4 : T // 2], 0)
        nc.vector.memset(vectors[:], 0.0)
        nc.vector.memset(w4_raw_scales[:].bitcast(I32), 0)
        make_identity(nc, identity[:])
        nc.gpsimd.memset(v2_scales[:].bitcast(I32), 0)
        nc.vector.memset(v3_scales[:].bitcast(I32), 0)

        def load_words(n, source, a):
            nc.sync.dma_start(words[n][a][:], source[a].rearrange("p t i -> p (t i)").bitcast(I32))

        def load_w1(a):
            nc.sync.dma_start(w1_raw[a][:], w1[K_PASS * a : K_PASS * (a + 1), :].rearrange("(p i) c -> p i c", i=PACK))

        def load_w4(b):
            cols = slice(K_PASS // 2 * b, K_PASS // 2 * (b + 1))
            nc.sync.dma_start(w4_raw[b][:], w4_words.bitcast(I32)[:, :, cols].rearrange("a p c -> p a c"))

        def load_gain(n, gain):
            nc.sync.dma_start(vectors[PASSES * n : PASSES * (n + 1), :], gain.rearrange("(b c) -> b c", b=PASSES))

        def load_planes_side_by_side(queue, tile, source):
            for r in range(4):
                queue.dma_start(
                    tile[:].bitcast(I32)[r:P:32, :].rearrange("q (a t) -> q a t", a=PASSES),
                    source.bitcast(I32)[:, r:16:4, :].rearrange("a q t -> q a t"),
                )

        def load_planes_stacked(queue, tile, source, first_row):
            for q in range(4):
                queue.dma_start(
                    tile[:].bitcast(I32)[32 * q + first_row : 32 * q + first_row + 8, :],
                    source.bitcast(I32)[:, 4 * q : 4 * q + 4, :],
                )

        V2_ROW, V3_ROW = 4, 8
        BASE_ROW = 2 * PASSES
        load_w4(0)
        nc.sync.dma_start(lists[0][:], offs)
        load_w4(1)
        load_planes_side_by_side(nc.sync, v_scales, tab_scales)
        load_words(0, tab_words, 0)
        load_gain(1, gain2)
        load_gain(0, gain1)
        load_planes_side_by_side(nc.sync, w4_raw_scales, w4_scales)
        load_words(0, tab_words, 1)

        turned = held.tile([P, PACK, P], F32, name="held0")
        for t in range(PACK):
            nc.tensor.transpose(turned[:, t, :], vectors[:, t:K_PASS:PACK], identity[:])
        nc.vector.tensor_copy(gains[:], turned[:, :, 0:BASE_ROW].rearrange("p t r -> p r t"))

        nc.sync.dma_start(lists[1][:], offs2)
        load_w1(0)
        nc.sync.dma_start(lists[2][:], offs3)
        nc.sync.dma_start(vectors[BASE_ROW : BASE_ROW + 1, :], base.rearrange("(o c) -> o c", o=1))
        load_w1(1)
        load_words(1, tab2_words, 0)
        load_words(1, tab2_words, 1)
        load_words(2, tab3_words, 0)
        load_words(2, tab3_words, 1)
        load_planes_stacked(nc.gpsimd, v2_scales, tab2_scales, V2_ROW)
        load_planes_stacked(nc.gpsimd, v3_scales, tab3_scales, V3_ROW)

        picked = {}
        v_planes = [kept([P, S], U8, "v_plane%d" % a) for a in range(PASSES)]
        v2_planes = kept([P, S], U8, "w4_raw_scales")

        def pick_words(n, a, slot):
            picked[n, a] = kept([P, S], U32, slot)
            nc.vector.tensor_copy(picked[n, a][:], words[n][a][:].bitcast(U32).indirect(lists[n][:]))

        def pick_plane(dst, window, n):
            nc.vector.tensor_copy(dst[:], window.indirect(lists[n][:]))

        w4_codes = [kept([P, PASSES, 2 * K_PASS], U8, "w4_codes%d" % b) for b in range(PASSES)]
        w4_planes = [kept([P, PASSES, K_PASS], U8, "w4_planes0"), kept([P, PASSES, K_PASS], U8, "words0_1")]

        def deal_w4(b):
            cols = slice(K_PASS * b, K_PASS * (b + 1))
            nc.vector.tensor_copy(
                w4_codes[b][:].bitcast(U16).rearrange("p a (t m) -> p a m t", t=PACK),
                w4_raw[b][:].bitcast(U16).rearrange("p a (m t) -> p a m t", t=PACK),
            )
            nc.vector.tensor_copy(
                w4_planes[b][:].rearrange("p a (t m) -> p a m t", t=PACK),
                w4_raw_scales[:].rearrange("p (a c) -> p a c", a=PASSES)[:, :, cols].rearrange("p a (m t) -> p a m t", t=PACK),
            )

        w1_rounded = [[kept([P, PACK * K_PASS], BF16, "w1_rounded%d_%d" % (a, b)) for b in range(PASSES)] for a in range(PASSES)]
        v3_planes = kept([P, S], U8, "w1_rounded0_0")
        w1_codes = {}
        w1_planes = [[kept([P, K_PASS], U8, "w1_planes%d_%d" % (a, b)) for b in range(PASSES)] for a in range(PASSES)]

        def round_w1(a, b, part, copy):
            copy(
                w1_rounded[a][b][:].rearrange("p (t m i) -> p m i t", t=PACK, i=PACK)[:, part],
                w1_raw[a][:, :, K_PASS * b : K_PASS * (b + 1)].rearrange("p i (m t) -> p m i t", t=PACK)[:, part],
            )

        def quantise_w1(a, b, slot):
            w1_codes[a, b] = kept([P, K_PASS], U32, slot)
            nc.vector.quantize_mx(w1_codes[a, b][:].bitcast(FP8X4), w1_planes[a][b][:], w1_rounded[a][b][:])

        h_codes = [[kept([P, S], U32, "h_codes%d_%d" % (n, b)) for b in range(PASSES)] for n in range(2)]
        h_planes = [[kept([P, S], U8, "h_planes%d_%d" % (n, b)) for b in range(PASSES)] for n in range(2)]

        def first_stage(n, b, half, slot):
            activated = kept([P, HALF, PACK], F32, "activated%d_%d_%d" % (n, b, half))
            passes = (1, 0) if (n, b, half) == (1, 0, 1) else (0, 1)
            for c in range(HALF // CHUNK):
                cols = slice(HALF * half + CHUNK * c, HALF * half + CHUNK * (c + 1))
                bank = ring.tile([P, PACK, CHUNK], F32, name="bank%d" % (2 * half + c))
                for a in passes:
                    for t in range(PACK):
                        if n == 0:
                            codes = w1_codes[a, b][:, P * t : P * (t + 1)].bitcast(FP8X4)
                            plane = w1_planes[a][b][:, P * t : P * (t + 1)]
                        else:
                            codes = w4_codes[b][:, a, 2 * P * t : 2 * P * (t + 1)].bitcast(FP4X4)
                            plane = w4_planes[b][:, a, P * t : P * (t + 1)]
                        nc.tensor.matmul_mx(
                            bank[:, t, :], lhsT=codes, lhsT_scale=plane,
                            rhs=picked[0, a][:, cols].bitcast(FP8X4), rhs_scale=v_planes[a][:, cols],
                            start=(a == passes[0] and t == 0), stop=(a == passes[-1] and t == PACK - 1),
                        )
                nc.scalar.activation(
                    activated[:, CHUNK * c : CHUNK * (c + 1), :], bank[:].rearrange("p t n -> p n t"),
                    ACT.Tanh if n == 0 else ACT.Gelu_apprx_tanh,
                )
            rounded = kept([P, HALF, PACK], BF16, slot)
            nc.vector.tensor_tensor(
                rounded[:], activated[:],
                gains[:, PASSES * n + b, :].unsqueeze(1).to_broadcast([P, HALF, PACK]), ALU.mult,
            )
            return rounded

        def quantise_h(n, b, half, rounded):
            cols = slice(HALF * half, HALF * (half + 1))
            nc.vector.quantize_mx(
                h_codes[n][b][:, cols].bitcast(FP8X4), h_planes[n][b][:, cols],
                rounded[:].rearrange("p n t -> p (n t)"),
            )

        def second_pass(dst, n, b, m, h, cols, start, stop):
            planes, row = (v2_planes, V2_ROW) if n == 1 else (v3_planes, V3_ROW)
            teams = slice(P * m, P * (m + 1))
            nc.tensor.matmul_mx(
                dst, lhsT=picked[n, b][:, teams].bitcast(FP8X4), lhsT_scale=planes[row + 4 * b : P, teams],
                rhs=h_codes[h][b][:, cols].bitcast(FP8X4), rhs_scale=h_planes[h][b][:, cols],
                start=start, stop=stop,
            )

        waiting = []

        def step(n, b, half, slot):
            rounded = first_stage(n, b, half, slot)
            if waiting:
                quantise_h(*waiting.pop())
            waiting.append((n, b, half, rounded))


        def own_score(m):
            bank = held.tile([P, S], F32, name="held%d" % m)
            flat = bank[:]
            for b in range(PASSES):
                second_pass(flat, 1, b, m, 1, slice(0, S), b == 0, b == PASSES - 1)
            nc.scalar.activation(own[:, m, :], flat, ACT.Identity, bias=base_col[:, m : m + 1])


        def joint_term(n, b, h, half, first, last):
            for g in range(2):
                for i in range(2):
                    second_pass(
                        joint[half][g][:, i, :], n, b, 2 * g + i, h, slice(HALF * half, HALF * (half + 1)),
                        first and i == 0, last and i == 1,
                    )

        pick_words(0, 0, "picked0_0")
        pick_plane(v_planes[0], v_scales[:, 0:T], 0)
        deal_w4(0)
        pick_plane(v_planes[1], v_scales[:, T : 2 * T], 0)
        pick_words(0, 1, "picked0_1")
        deal_w4(1)
        pick_plane(v2_planes, v2_scales[:], 1)
        for b in range(PASSES):
            for half in range(2):
                step(1, b, half, "rounded%d_%d" % (b, half))
        quantise_h(*waiting.pop())

        turned = held.tile([P, S // P, P], F32, name="held1")
        for m in range(S // P):
            nc.tensor.transpose(turned[:, m, :], vectors[:, P * m : P * (m + 1)], identity[:])
        nc.vector.tensor_copy(base_col[:], turned[:, :, BASE_ROW])

        round_w1(0, 0, slice(0, P), nc.scalar.copy)
        quantise_w1(0, 0, "w1_codes0_0")
        pick_plane(v3_planes, v3_scales[:], 2)
        round_w1(0, 1, slice(0, P), nc.scalar.copy)
        pick_words(1, 0, "picked1_0")
        quantise_w1(0, 1, "words1_0")
        round_w1(1, 0, slice(0, SPLIT), nc.scalar.copy)
        round_w1(1, 0, slice(SPLIT, P), nc.vector.tensor_copy)
        pick_words(1, 1, "picked1_1")
        quantise_w1(1, 0, "words1_1")
        round_w1(1, 1, slice(0, P), nc.scalar.copy)
        own = kept([P, S // P, S], F32, "own")
        for m in range(S // P):
            own_score(m)
        joint = [[held.tile([P, 2, HALF], F32, name="held%d" % (2 * half + g)) for g in range(2)] for half in range(2)]
        pick_words(2, 0, "picked2_0")
        quantise_w1(1, 1, "words2_0")
        pick_words(2, 1, "picked2_1")
        step(0, 0, 0, "words2_1")
        step(0, 0, 1, "activated0_0_0")
        step(0, 1, 0, "activated0_0_1")
        step(0, 1, 1, "activated0_1_0")
        quantise_h(*waiting.pop())
        terms = ((2, 0, 1), (2, 1, 1), (1, 0, 0), (1, 1, 0))
        for k, (n, b, h) in enumerate(terms):
            for half in range(2):
                joint_term(n, b, h, half, k == 0, k == len(terms) - 1)

        for half in range(2):
            cols = slice(HALF * half, HALF * (half + 1))
            for g in range(2):
                scores = kept([P, 2, HALF], F32, "scores%d_%d" % (half, g))
                for i in range(2):
                    m = 2 * g + i
                    nc.vector.scalar_tensor_tensor(
                        scores[:, i, :], joint[half][g][:, i, :], base_col[:, m : m + 1], own[:, m, cols],
                        ALU.add, ALU.max,
                    )
                nc.sync.dma_start(
                    out[2 * P * g : 2 * P * (g + 1), cols].rearrange("(i p) j -> p i j", p=P), scores[:],
                )
